import numpy as np
import ml_dtypes


def mxq(x, axis, fmt="e4m3"):
    dtype, down = {"e4m3": (ml_dtypes.float8_e4m3fn, 7), "e5m2": (ml_dtypes.float8_e5m2, 14)}[fmt]
    v = np.moveaxis(np.asarray(x, np.float32).astype(ml_dtypes.bfloat16).astype(np.float64), axis, -1)
    blocks = v.reshape(v.shape[:-1] + (-1, 32))
    amax = np.abs(blocks).max(-1, keepdims=True)
    byte = np.maximum(np.where(amax > 0, np.frexp(amax)[1] - 1 + 127, 0) - down, 1)
    scale = np.exp2(byte - 127.0)
    codes = (blocks / scale).astype(np.float32).astype(dtype).astype(np.float64)
    return np.moveaxis((codes * scale).reshape(v.shape), -1, axis)


WIDE = False


def mx_kscale(k):
    if not WIDE:
        return np.ones(k)
    levels = np.array([10, -10, 5, -5, 0])
    if k % 512:
        return np.exp2(np.random.permutation(np.resize(levels, k // 32))).repeat(32)
    a = np.empty((k // 512, 16))
    for p in range(k // 512):
        a[p, :8] = np.random.permutation(np.resize(levels, 8))
        for g in range(8):
            far = levels[np.abs(levels - a[p, g]) >= 10]
            a[p, g + 8] = far[np.random.randint(len(far))]
    return np.exp2(a.ravel()).repeat(32)


def f64(x):
    return np.asarray(x).astype(np.float64)


def striped8(idx):
    return np.asarray(idx).reshape(8, -1, 16).transpose(0, 2, 1).reshape(128, -1).astype(np.uint16)


def unstriped8(offs):
    return offs.reshape(8, 16, -1).transpose(0, 2, 1).reshape(8, -1).astype(np.int64)


def pick8(x, idx, run):
    r = np.arange(len(x))
    return x[r[:, None], idx[r % (8 * run) // run]]


E2M1 = np.array([0.0, 0.5, 1.0, 1.5, 2.0, 3.0, 4.0, 6.0, -0.0, -0.5, -1.0, -1.5, -2.0, -3.0, -4.0, -6.0])


def pack_weight(w, fmt):
    k, n = w.shape
    w = f64(np.asarray(w, np.float32).astype(ml_dtypes.bfloat16)).reshape(k // 32, 32, n)
    amax = np.abs(w).max(1)
    if fmt == "e4m3":
        byte = np.frexp(amax)[1] - 1 + 127 - 7
    else:
        mant, ex = np.frexp(amax / 6.0)
        byte = np.where(mant > 0.5, ex, ex - 1) + 127
    byte = np.clip(np.where(amax > 0, byte, 1), 1, 254)
    scaled = (w * np.exp2(127.0 - byte)[:, None, :]).reshape(k, n).astype(np.float32)
    by_word = np.ascontiguousarray(scaled.reshape(k // 512, 128, 4, n).transpose(0, 1, 3, 2))
    if fmt == "e4m3":
        words = by_word.astype(ml_dtypes.float8_e4m3fn).view(np.uint8)
    else:
        c = by_word.astype(ml_dtypes.float4_e2m1fn).view(np.uint8) & 0xF
        words = (c[..., 0::2] | (c[..., 1::2] << 4)).reshape(k // 512, 128, 2 * n)
    return np.ascontiguousarray(words), np.ascontiguousarray(byte.astype(np.uint8).reshape(k // 512, 16, n))


def unpack_weight(words, scales, fmt):
    g, _, n = scales.shape
    words = np.ascontiguousarray(words).reshape(g, 128, n, -1)
    if fmt == "e4m3":
        vals = words.view(ml_dtypes.float8_e4m3fn).astype(np.float64)
    else:
        nib = np.empty((g, 128, n, 4), np.uint8)
        nib[..., 0::2] = words & 0xF
        nib[..., 1::2] = words >> 4
        vals = E2M1[nib]
    vals = vals * np.repeat(np.exp2(scales.astype(np.float64) - 127.0), 8, axis=1)[..., None]
    return vals.transpose(0, 1, 3, 2).reshape(g * 512, n)


D, T, I, Q = 512, 1024, 512, 128


def setup_inputs():
    n = np.random.standard_normal
    idx = np.stack([np.random.permutation(T)[:I] for _ in range(8)])
    idx2 = np.stack([np.random.permutation(T)[:I] for _ in range(8)])
    idx3 = np.stack([np.random.permutation(T)[:I] for _ in range(8)])
    fd = mx_kscale(D)
    keysp = pack_weight(n((D, T)) / fd[:, None], "e4m3")
    return {
        "query": (n((D, Q)) * 1.0 / np.sqrt(D) * fd[:, None]).astype(np.float32),
        "keys_words": keysp[0],
        "keys_scales": keysp[1],
        "old": (1.0 * n((Q, T))).astype(np.float32),
        "offs": striped8(idx),
        "offs2": striped8(idx2),
        "offs3": striped8(idx3),
    }


def reference(query, keys_words, keys_scales, old, offs, offs2, offs3):
    idx = unstriped8(offs)
    idx2 = unstriped8(offs2)
    idx3 = unstriped8(offs3)
    keysu = unpack_weight(keys_words, keys_scales, "e4m3")
    queryq = mxq(f64(query), 0, "e4m3")
    a = queryq.T @ keysu
    s = pick8(a, idx, 16) - pick8(a, idx2, 16)
    p = np.exp(s - np.max(s, axis=1, keepdims=True))
    w = p / np.sum(p, axis=1, keepdims=True)
    ws = w * 256.0
    f1 = np.zeros((Q, T))
    f1[np.arange(Q)[:, None], idx[np.arange(Q) % 128 // 16]] = ws
    f2 = f1 + f64(old)
    y = pick8(f2, idx3, 16)
    return y

@@ -1,0 +1,131 @@
+from contextlib import ExitStack
+
+import concourse.mybir as mybir
+
+D, T, I, Q = 512, 1024, 512, 128
+FLOPS = 2 * D * Q * T
+
+F32 = mybir.dt.float32
+BF16 = mybir.dt.bfloat16
+I32 = mybir.dt.int32
+U32 = mybir.dt.uint32
+U16 = mybir.dt.uint16
+U8 = mybir.dt.uint8
+FP8X4 = mybir.dt.float8_e4m3fn_x4
+ALU = mybir.AluOpType
+ACT = mybir.ActivationFunctionType
+
+P = 128
+PACK = 4
+HALF = I // 2
+LIST_COLS = I // 16
+HALF_COLS = LIST_COLS // 2
+KEY_HALF = T // 2
+N_MM = 256
+
+
+def tile_attend_difference_soft_through_heads_kernel(tc, query, keys_words, keys_scales, old, offs, offs2, offs3, out):
+    nc = tc.nc
+    with ExitStack() as ctx:
+        sb = ctx.enter_context(tc.tile_pool(name="sb", bufs=1))
+        psum = ctx.enter_context(tc.psum_pool(name="psum", bufs=1))
+
+        list1 = sb.tile([P, LIST_COLS], U16)
+        list2 = sb.tile([P, LIST_COLS], U16)
+        list3 = sb.tile([P, LIST_COLS], U16)
+
+        q_raw = sb.tile([P, PACK, Q], F32, tag="loaded")
+        nc.sync.dma_start(out=q_raw[:], in_=query.rearrange("(p j) q -> p j q", j=PACK))
+
+        k_scales = sb.tile([P, T], U8, align_bytes=64)
+        for quad in range(4):
+            nc.scalar.dma_start(
+                out=k_scales[32 * quad : 32 * quad + 4, :].bitcast(I32),
+                in_=keys_scales[0, 4 * quad : 4 * quad + 4, :].bitcast(I32),
+            )
+
+        words_hbm = keys_words[0].rearrange("p n t -> p (n t)")
+        k_words = []
+        for h in range(2):
+            half = sb.tile([P, KEY_HALF], U32, align_bytes=64, name="k_words%d" % h)
+            nc.sync.dma_start(
+                out=half[:].bitcast(I32),
+                in_=words_hbm[:, h * KEY_HALF * PACK : (h + 1) * KEY_HALF * PACK].bitcast(I32),
+            )
+            k_words.append(half)
+
+        nc.sync.dma_start(list2[:], offs2)
+        nc.sync.dma_start(list1[:], offs)
+        nc.sync.dma_start(list3[:], offs3)
+
+        f1 = sb.tile([P, T], F32)
+        nc.gpsimd.memset(f1[:], 0.0)
+
+        q_bf = sb.tile([P, Q, PACK], BF16, align_bytes=64)
+        nc.vector.tensor_copy(
+            out=q_bf[:].rearrange("p (c i) t -> p c t i", i=4),
+            in_=q_raw[:].rearrange("p t (c i) -> p c t i", i=4),
+        )
+        q_codes = sb.tile([P, Q], U32, align_bytes=64)
+        q_scales = sb.tile([P, Q], U8, align_bytes=64)
+        nc.vector.quantize_mx(
+            out=q_codes[:].bitcast(FP8X4), scales=q_scales[:], in_=q_bf[:].rearrange("p q t -> p (q t)")
+        )
+
+        old_sb = sb.tile([P, T], F32, tag="loaded")
+        nc.sync.dma_start(out=old_sb[:], in_=old)
+
+        a = sb.tile([P, T], F32)
+        for b in range(T // N_MM):
+            bank = psum.tile([P, N_MM], F32, name="bank%d" % b)
+            h, c0 = divmod(b * N_MM, KEY_HALF)
+            cols = slice(b * N_MM, (b + 1) * N_MM)
+            nc.tensor.matmul_mx(
+                out=bank[:],
+                lhsT=q_codes[:].bitcast(FP8X4),
+                lhsT_scale=q_scales[:],
+                rhs=k_words[h][:, c0 : c0 + N_MM].bitcast(FP8X4),
+                rhs_scale=k_scales[:, cols],
+                start=True,
+                stop=True,
+            )
+            if b % 2 == 0:
+                nc.scalar.copy(out=a[:, cols], in_=bank[:])
+            else:
+                nc.vector.tensor_copy(out=a[:, cols], in_=bank[:])
+
+        first = slice(0, HALF_COLS)
+        second = slice(HALF_COLS, LIST_COLS)
+        lo = slice(0, HALF)
+        hi = slice(HALF, I)
+
+        a2_lo = sb.tile([P, HALF], F32)
+        a2_hi = sb.tile([P, HALF], F32)
+        a1_hi = sb.tile([P, HALF], F32)
+        s = sb.tile([P, I], F32)
+        nc.scalar.activation(a2_lo[:], a[:].indirect(list2[:, first]), ACT.Copy)
+        nc.vector.tensor_copy(a1_hi[:], a[:].indirect(list1[:, second]))
+        nc.scalar.activation(a2_hi[:], a[:].indirect(list2[:, second]), ACT.Copy)
+        nc.vector.tensor_tensor(s[:, lo], a[:].indirect(list1[:, first]), a2_lo[:], ALU.subtract)
+        nc.vector.tensor_tensor(s[:, hi], a1_hi[:], a2_hi[:], ALU.subtract)
+
+        neg_max = sb.tile([P, 1], F32)
+        nc.vector.tensor_reduce(neg_max[:], s[:], mybir.AxisListType.X, ALU.max, negate=True)
+        p = sb.tile([P, I], F32)
+        total = sb.tile([P, 1], F32)
+        nc.scalar.activation(p[:], s[:], ACT.Exp, bias=neg_max[:], scale=1.0, accum_out=total[:])
+        inv = sb.tile([P, 1], F32)
+        nc.vector.reciprocal(inv[:], total[:])
+        ws = sb.tile([P, I], F32)
+        nc.vector.tensor_scalar(ws[:], p[:], inv[:], 256.0, ALU.mult, ALU.mult)
+
+        nc.vector.tensor_copy(f1[:].indirect(list1[:]), ws[:])
+        f2 = sb.tile([P, T], F32)
+        nc.vector.tensor_tensor(f2[:], f1[:], old_sb[:], ALU.add)
+
+        y_lo = sb.tile([P, HALF], F32)
+        y_hi = sb.tile([P, HALF], F32)
+        nc.vector.tensor_copy(y_lo[:], f2[:].indirect(list3[:, first]))
+        nc.scalar.activation(y_hi[:], f2[:].indirect(list3[:, second]), ACT.Copy)
+        nc.sync.dma_start(out=out[:, lo], in_=y_lo[:])
+        nc.scalar.dma_start(out=out[:, hi], in_=y_hi[:])

@@ -21,7 +21,7 @@ HALF = I // 2
 LIST_COLS = I // 16
 HALF_COLS = LIST_COLS // 2
 KEY_HALF = T // 2
-N_MM = 256
+MM_WIDTHS = (256, 256, 256, 128, 128)
 
 
 def tile_attend_difference_soft_through_heads_kernel(tc, query, keys_words, keys_scales, old, offs, offs2, offs3, out):
@@ -39,7 +39,8 @@ def tile_attend_difference_soft_through_heads_kernel(tc, query, keys_words, keys
 
         k_scales = sb.tile([P, T], U8, align_bytes=64)
         for quad in range(4):
-            nc.scalar.dma_start(
+            queue = nc.scalar if quad < 2 else nc.sync
+            queue.dma_start(
                 out=k_scales[32 * quad : 32 * quad + 4, :].bitcast(I32),
                 in_=keys_scales[0, 4 * quad : 4 * quad + 4, :].bitcast(I32),
             )
@@ -59,32 +60,38 @@ def tile_attend_difference_soft_through_heads_kernel(tc, query, keys_words, keys
         nc.sync.dma_start(list3[:], offs3)
 
         f1 = sb.tile([P, T], F32)
-        nc.gpsimd.memset(f1[:], 0.0)
+        nc.vector.memset(f1[:], 0.0)
 
         q_bf = sb.tile([P, Q, PACK], BF16, align_bytes=64)
-        nc.vector.tensor_copy(
-            out=q_bf[:].rearrange("p (c i) t -> p c t i", i=4),
-            in_=q_raw[:].rearrange("p t (c i) -> p c t i", i=4),
-        )
         q_codes = sb.tile([P, Q], U32, align_bytes=64)
         q_scales = sb.tile([P, Q], U8, align_bytes=64)
-        nc.vector.quantize_mx(
-            out=q_codes[:].bitcast(FP8X4), scales=q_scales[:], in_=q_bf[:].rearrange("p q t -> p (q t)")
-        )
+        q_halves = (slice(0, Q // 2), slice(Q // 2, Q))
+        for rows in q_halves:
+            nc.vector.tensor_copy(
+                out=q_bf[:, rows, :].rearrange("p (c i) t -> p c t i", i=4),
+                in_=q_raw[:, :, rows].rearrange("p t (c i) -> p c t i", i=4),
+            )
+        for rows in q_halves:
+            nc.vector.quantize_mx(
+                out=q_codes[:, rows].bitcast(FP8X4),
+                scales=q_scales[:, rows],
+                in_=q_bf[:, rows, :].rearrange("p q t -> p (q t)"),
+            )
 
         old_sb = sb.tile([P, T], F32, tag="loaded")
         nc.sync.dma_start(out=old_sb[:], in_=old)
 
         a = sb.tile([P, T], F32)
-        for b in range(T // N_MM):
-            bank = psum.tile([P, N_MM], F32, name="bank%d" % b)
-            h, c0 = divmod(b * N_MM, KEY_HALF)
-            cols = slice(b * N_MM, (b + 1) * N_MM)
+        for b, width in enumerate(MM_WIDTHS):
+            bank = psum.tile([P, width], F32, name="bank%d" % b)
+            t0 = sum(MM_WIDTHS[:b])
+            h, c0 = divmod(t0, KEY_HALF)
+            cols = slice(t0, t0 + width)
             nc.tensor.matmul_mx(
                 out=bank[:],
                 lhsT=q_codes[:].bitcast(FP8X4),
                 lhsT_scale=q_scales[:],
-                rhs=k_words[h][:, c0 : c0 + N_MM].bitcast(FP8X4),
+                rhs=k_words[h][:, c0 : c0 + width].bitcast(FP8X4),
                 rhs_scale=k_scales[:, cols],
                 start=True,
                 stop=True,

@@ -1,6 +1,7 @@
 from contextlib import ExitStack
 
 import concourse.mybir as mybir
+from concourse.masks import make_identity
 
 D, T, I, Q = 512, 1024, 512, 128
 FLOPS = 2 * D * Q * T
@@ -21,6 +22,9 @@ HALF = I // 2
 LIST_COLS = I // 16
 HALF_COLS = LIST_COLS // 2
 KEY_HALF = T // 2
+VEC_COLS = 640
+PLANE = T // 4
+GP_START = 640
 MM_WIDTHS = (256, 256, 256, 128, 128)
 
 
@@ -37,12 +41,12 @@ def tile_attend_difference_soft_through_heads_kernel(tc, query, keys_words, keys
         q_raw = sb.tile([P, PACK, Q], F32, tag="loaded")
         nc.sync.dma_start(out=q_raw[:], in_=query.rearrange("(p j) q -> p j q", j=PACK))
 
-        k_scales = sb.tile([P, T], U8, align_bytes=64)
+        k_scales = sb.tile([P, PLANE], U8, align_bytes=64)
         for quad in range(4):
             queue = nc.scalar if quad < 2 else nc.sync
             queue.dma_start(
-                out=k_scales[32 * quad : 32 * quad + 4, :].bitcast(I32),
-                in_=keys_scales[0, 4 * quad : 4 * quad + 4, :].bitcast(I32),
+                out=k_scales[32 * quad : 32 * quad + 16, :].bitcast(I32),
+                in_=keys_scales[0, 4 * quad : 4 * quad + 4, :].bitcast(I32).rearrange("j (g c) -> g j c", g=4),
             )
 
         words_hbm = keys_words[0].rearrange("p n t -> p (n t)")
@@ -83,16 +87,17 @@ def tile_attend_difference_soft_through_heads_kernel(tc, query, keys_words, keys
 
         a = sb.tile([P, T], F32)
         for b, width in enumerate(MM_WIDTHS):
-            bank = psum.tile([P, width], F32, name="bank%d" % b)
+            bank = psum.tile([P, width], F32, name="bank", tag="bank%d" % b)
             t0 = sum(MM_WIDTHS[:b])
             h, c0 = divmod(t0, KEY_HALF)
+            plane, s0 = divmod(t0, PLANE)
             cols = slice(t0, t0 + width)
             nc.tensor.matmul_mx(
                 out=bank[:],
                 lhsT=q_codes[:].bitcast(FP8X4),
                 lhsT_scale=q_scales[:],
                 rhs=k_words[h][:, c0 : c0 + width].bitcast(FP8X4),
-                rhs_scale=k_scales[:, cols],
+                rhs_scale=k_scales[4 * plane : P, s0 : s0 + width],
                 start=True,
                 stop=True,
             )
@@ -109,7 +114,7 @@ def tile_attend_difference_soft_through_heads_kernel(tc, query, keys_words, keys
         a2_lo = sb.tile([P, HALF], F32)
         a2_hi = sb.tile([P, HALF], F32)
         a1_hi = sb.tile([P, HALF], F32)
-        s = sb.tile([P, I], F32)
+        s = sb.tile([P, I], F32, tag="scores")
         nc.scalar.activation(a2_lo[:], a[:].indirect(list2[:, first]), ACT.Copy)
         nc.vector.tensor_copy(a1_hi[:], a[:].indirect(list1[:, second]))
         nc.scalar.activation(a2_hi[:], a[:].indirect(list2[:, second]), ACT.Copy)
@@ -121,6 +126,20 @@ def tile_attend_difference_soft_through_heads_kernel(tc, query, keys_words, keys
         p = sb.tile([P, I], F32)
         total = sb.tile([P, 1], F32)
         nc.scalar.activation(p[:], s[:], ACT.Exp, bias=neg_max[:], scale=1.0, accum_out=total[:])
+        ident = sb.tile([P, P], F32)
+        make_identity(nc, ident[:])
+        old_t = sb.tile([P, VEC_COLS], F32, tag="scores")
+        old_psum = []
+        for n, (c0, c1) in enumerate(((0, 512), (512, VEC_COLS))):
+            turned = psum.tile([P, c1 - c0], F32, name="turned", tag="bank%d" % (3 + n))
+            for c in range(c0, c1, P):
+                nc.tensor.transpose(turned[:, c - c0 : c - c0 + P], old_sb[:, c : c + P], ident[:])
+            nc.scalar.copy(out=old_t[:, c0:c1], in_=turned[:])
+            back = psum.tile([P, c1 - c0], F32, name="back", tag="back%d" % n)
+            for c in range(c0, c1, P):
+                nc.tensor.transpose(back[:, c - c0 : c - c0 + P], old_t[:, c : c + P], ident[:])
+            old_psum.append((c0, c1, back))
+
         inv = sb.tile([P, 1], F32)
         nc.vector.reciprocal(inv[:], total[:])
         ws = sb.tile([P, I], F32)
@@ -128,7 +147,10 @@ def tile_attend_difference_soft_through_heads_kernel(tc, query, keys_words, keys
 
         nc.vector.tensor_copy(f1[:].indirect(list1[:]), ws[:])
         f2 = sb.tile([P, T], F32)
-        nc.vector.tensor_tensor(f2[:], f1[:], old_sb[:], ALU.add)
+        for c0, c1, bank in old_psum:
+            c1 = min(c1, GP_START)
+            nc.vector.tensor_tensor(f2[:, c0:c1], f1[:, c0:c1], bank[:, : c1 - c0], ALU.add)
+        nc.gpsimd.tensor_tensor(f2[:, GP_START:], f1[:, GP_START:], old_sb[:, GP_START:], ALU.add)
 
         y_lo = sb.tile([P, HALF], F32)
         y_hi = sb.tile([P, HALF], F32)

from contextlib import ExitStack

import concourse.mybir as mybir
from concourse.masks import make_identity

D, T, I, Q = 512, 1024, 512, 128
FLOPS = 2 * D * Q * T

F32 = mybir.dt.float32
BF16 = mybir.dt.bfloat16
I32 = mybir.dt.int32
U32 = mybir.dt.uint32
U16 = mybir.dt.uint16
U8 = mybir.dt.uint8
FP8X4 = mybir.dt.float8_e4m3fn_x4
ALU = mybir.AluOpType
ACT = mybir.ActivationFunctionType

P = 128
PACK = 4
HALF = I // 2
LIST_COLS = I // 16
HALF_COLS = LIST_COLS // 2
KEY_HALF = T // 2
VEC_COLS = 640
PLANE = T // 4
GP_START = 640
MM_WIDTHS = (256, 256, 256, 128, 128)


def tile_attend_difference_soft_through_heads_kernel(tc, query, keys_words, keys_scales, old, offs, offs2, offs3, out):
    nc = tc.nc
    with ExitStack() as ctx:
        sb = ctx.enter_context(tc.tile_pool(name="sb", bufs=1))
        psum = ctx.enter_context(tc.psum_pool(name="psum", bufs=1))

        list1 = sb.tile([P, LIST_COLS], U16)
        list2 = sb.tile([P, LIST_COLS], U16)
        list3 = sb.tile([P, LIST_COLS], U16)

        q_raw = sb.tile([P, PACK, Q], F32, tag="loaded")
        nc.sync.dma_start(out=q_raw[:], in_=query.rearrange("(p j) q -> p j q", j=PACK))

        k_scales = sb.tile([P, PLANE], U8, align_bytes=64)
        for quad in range(4):
            queue = nc.scalar if quad < 2 else nc.sync
            queue.dma_start(
                out=k_scales[32 * quad : 32 * quad + 16, :].bitcast(I32),
                in_=keys_scales[0, 4 * quad : 4 * quad + 4, :].bitcast(I32).rearrange("j (g c) -> g j c", g=4),
            )

        words_hbm = keys_words[0].rearrange("p n t -> p (n t)")
        k_words = []
        for h in range(2):
            half = sb.tile([P, KEY_HALF], U32, align_bytes=64, name="k_words%d" % h)
            nc.sync.dma_start(
                out=half[:].bitcast(I32),
                in_=words_hbm[:, h * KEY_HALF * PACK : (h + 1) * KEY_HALF * PACK].bitcast(I32),
            )
            k_words.append(half)

        nc.sync.dma_start(list2[:], offs2)
        nc.sync.dma_start(list1[:], offs)
        nc.sync.dma_start(list3[:], offs3)

        f1 = sb.tile([P, T], F32)
        nc.vector.memset(f1[:], 0.0)

        q_bf = sb.tile([P, Q, PACK], BF16, align_bytes=64)
        q_codes = sb.tile([P, Q], U32, align_bytes=64)
        q_scales = sb.tile([P, Q], U8, align_bytes=64)
        q_halves = (slice(0, Q // 2), slice(Q // 2, Q))
        for rows in q_halves:
            nc.vector.tensor_copy(
                out=q_bf[:, rows, :].rearrange("p (c i) t -> p c t i", i=4),
                in_=q_raw[:, :, rows].rearrange("p t (c i) -> p c t i", i=4),
            )
        for rows in q_halves:
            nc.vector.quantize_mx(
                out=q_codes[:, rows].bitcast(FP8X4),
                scales=q_scales[:, rows],
                in_=q_bf[:, rows, :].rearrange("p q t -> p (q t)"),
            )

        old_sb = sb.tile([P, T], F32, tag="loaded")
        nc.sync.dma_start(out=old_sb[:], in_=old)

        a = sb.tile([P, T], F32)
        for b, width in enumerate(MM_WIDTHS):
            bank = psum.tile([P, width], F32, name="bank", tag="bank%d" % b)
            t0 = sum(MM_WIDTHS[:b])
            h, c0 = divmod(t0, KEY_HALF)
            plane, s0 = divmod(t0, PLANE)
            cols = slice(t0, t0 + width)
            nc.tensor.matmul_mx(
                out=bank[:],
                lhsT=q_codes[:].bitcast(FP8X4),
                lhsT_scale=q_scales[:],
                rhs=k_words[h][:, c0 : c0 + width].bitcast(FP8X4),
                rhs_scale=k_scales[4 * plane : P, s0 : s0 + width],
                start=True,
                stop=True,
            )
            if b % 2 == 0:
                nc.scalar.copy(out=a[:, cols], in_=bank[:])
            else:
                nc.vector.tensor_copy(out=a[:, cols], in_=bank[:])

        first = slice(0, HALF_COLS)
        second = slice(HALF_COLS, LIST_COLS)
        lo = slice(0, HALF)
        hi = slice(HALF, I)

        a2_lo = sb.tile([P, HALF], F32)
        a2_hi = sb.tile([P, HALF], F32)
        a1_hi = sb.tile([P, HALF], F32)
        s = sb.tile([P, I], F32, tag="scores")
        nc.scalar.activation(a2_lo[:], a[:].indirect(list2[:, first]), ACT.Copy)
        nc.vector.tensor_copy(a1_hi[:], a[:].indirect(list1[:, second]))
        nc.scalar.activation(a2_hi[:], a[:].indirect(list2[:, second]), ACT.Copy)
        nc.vector.tensor_tensor(s[:, lo], a[:].indirect(list1[:, first]), a2_lo[:], ALU.subtract)
        nc.vector.tensor_tensor(s[:, hi], a1_hi[:], a2_hi[:], ALU.subtract)

        neg_max = sb.tile([P, 1], F32)
        nc.vector.tensor_reduce(neg_max[:], s[:], mybir.AxisListType.X, ALU.max, negate=True)
        p = sb.tile([P, I], F32)
        total = sb.tile([P, 1], F32)
        nc.scalar.activation(p[:], s[:], ACT.Exp, bias=neg_max[:], scale=1.0, accum_out=total[:])
        ident = sb.tile([P, P], F32)
        make_identity(nc, ident[:])
        old_t = sb.tile([P, VEC_COLS], F32, tag="scores")
        old_psum = []
        for n, (c0, c1) in enumerate(((0, 512), (512, VEC_COLS))):
            turned = psum.tile([P, c1 - c0], F32, name="turned", tag="bank%d" % (3 + n))
            for c in range(c0, c1, P):
                nc.tensor.transpose(turned[:, c - c0 : c - c0 + P], old_sb[:, c : c + P], ident[:])
            nc.scalar.copy(out=old_t[:, c0:c1], in_=turned[:])
            back = psum.tile([P, c1 - c0], F32, name="back", tag="back%d" % n)
            for c in range(c0, c1, P):
                nc.tensor.transpose(back[:, c - c0 : c - c0 + P], old_t[:, c : c + P], ident[:])
            old_psum.append((c0, c1, back))

        inv = sb.tile([P, 1], F32)
        nc.vector.reciprocal(inv[:], total[:])
        ws = sb.tile([P, I], F32)
        nc.vector.tensor_scalar(ws[:], p[:], inv[:], 256.0, ALU.mult, ALU.mult)

        nc.vector.tensor_copy(f1[:].indirect(list1[:]), ws[:])
        f2 = sb.tile([P, T], F32)
        for c0, c1, bank in old_psum:
            c1 = min(c1, GP_START)
            nc.vector.tensor_tensor(f2[:, c0:c1], f1[:, c0:c1], bank[:, : c1 - c0], ALU.add)
        nc.gpsimd.tensor_tensor(f2[:, GP_START:], f1[:, GP_START:], old_sb[:, GP_START:], ALU.add)

        y_lo = sb.tile([P, HALF], F32)
        y_hi = sb.tile([P, HALF], F32)
        nc.vector.tensor_copy(y_lo[:], f2[:].indirect(list3[:, first]))
        nc.scalar.activation(y_hi[:], f2[:].indirect(list3[:, second]), ACT.Copy)
        nc.sync.dma_start(out=out[:, lo], in_=y_lo[:])
        nc.scalar.dma_start(out=out[:, hi], in_=y_hi[:])
